import numpy as np
import ml_dtypes


def mxq(x, axis, fmt="e4m3"):
    dtype, down = {"e4m3": (ml_dtypes.float8_e4m3fn, 7), "e5m2": (ml_dtypes.float8_e5m2, 14)}[fmt]
    v = np.moveaxis(np.asarray(x, np.float32).astype(ml_dtypes.bfloat16).astype(np.float64), axis, -1)
    blocks = v.reshape(v.shape[:-1] + (-1, 32))
    amax = np.abs(blocks).max(-1, keepdims=True)
    byte = np.maximum(np.where(amax > 0, np.frexp(amax)[1] - 1 + 127, 0) - down, 1)
    scale = np.exp2(byte - 127.0)
    codes = (blocks / scale).astype(np.float32).astype(dtype).astype(np.float64)
    return np.moveaxis((codes * scale).reshape(v.shape), -1, axis)


WIDE = False


def mx_kscale(k):
    if not WIDE:
        return np.ones(k)
    levels = np.array([10, -10, 5, -5, 0])
    if k % 512:
        return np.exp2(np.random.permutation(np.resize(levels, k // 32))).repeat(32)
    a = np.empty((k // 512, 16))
    for p in range(k // 512):
        a[p, :8] = np.random.permutation(np.resize(levels, 8))
        for g in range(8):
            far = levels[np.abs(levels - a[p, g]) >= 10]
            a[p, g + 8] = far[np.random.randint(len(far))]
    return np.exp2(a.ravel()).repeat(32)


def f64(x):
    return np.asarray(x).astype(np.float64)


def striped(idx):
    return np.tile(np.asarray(idx).reshape(-1, 16).T, (8, 1)).astype(np.uint16)


def unstriped(offs):
    return offs[:16].T.reshape(-1).astype(np.int64)


E2M1 = np.array([0.0, 0.5, 1.0, 1.5, 2.0, 3.0, 4.0, 6.0, -0.0, -0.5, -1.0, -1.5, -2.0, -3.0, -4.0, -6.0])


def pack_weight(w, fmt):
    k, n = w.shape
    w = f64(np.asarray(w, np.float32).astype(ml_dtypes.bfloat16)).reshape(k // 32, 32, n)
    amax = np.abs(w).max(1)
    if fmt == "e4m3":
        byte = np.frexp(amax)[1] - 1 + 127 - 7
    else:
        mant, ex = np.frexp(amax / 6.0)
        byte = np.where(mant > 0.5, ex, ex - 1) + 127
    byte = np.clip(np.where(amax > 0, byte, 1), 1, 254)
    scaled = (w * np.exp2(127.0 - byte)[:, None, :]).reshape(k, n).astype(np.float32)
    by_word = np.ascontiguousarray(scaled.reshape(k // 512, 128, 4, n).transpose(0, 1, 3, 2))
    if fmt == "e4m3":
        words = by_word.astype(ml_dtypes.float8_e4m3fn).view(np.uint8)
    else:
        c = by_word.astype(ml_dtypes.float4_e2m1fn).view(np.uint8) & 0xF
        words = (c[..., 0::2] | (c[..., 1::2] << 4)).reshape(k // 512, 128, 2 * n)
    return np.ascontiguousarray(words), np.ascontiguousarray(byte.astype(np.uint8).reshape(k // 512, 16, n))


def unpack_weight(words, scales, fmt):
    g, _, n = scales.shape
    words = np.ascontiguousarray(words).reshape(g, 128, n, -1)
    if fmt == "e4m3":
        vals = words.view(ml_dtypes.float8_e4m3fn).astype(np.float64)
    else:
        nib = np.empty((g, 128, n, 4), np.uint8)
        nib[..., 0::2] = words & 0xF
        nib[..., 1::2] = words >> 4
        vals = E2M1[nib]
    vals = vals * np.repeat(np.exp2(scales.astype(np.float64) - 127.0), 8, axis=1)[..., None]
    return vals.transpose(0, 1, 3, 2).reshape(g * 512, n)


def sigmoid(v):
    return 1.0 / (1.0 + np.exp(-v))


D, E, T, I, Q = 512, 512, 2048, 512, 128


def setup_inputs():
    n = np.random.standard_normal
    idx = np.random.permutation(T)[:I]
    fd = mx_kscale(D)
    fe = mx_kscale(E)
    keysp = pack_weight(n((D, T)) / fd[:, None], "e4m3")
    valsp = pack_weight(n((E, T)) / fe[:, None], "e4m3")
    return {
        "query": (n((D, Q)) * 0.5 / np.sqrt(D) * fd[:, None]).astype(np.float32),
        "query2": (n((D, Q)) * 0.8 / np.sqrt(D) * fd[:, None]).astype(np.float32),
        "keys_words": keysp[0],
        "keys_scales": keysp[1],
        "gout": (n((E, Q)) * 1 / np.sqrt(E) * fe[:, None]).astype(np.float32),
        "vals_words": valsp[0],
        "vals_scales": valsp[1],
        "size": (np.random.uniform(0.5, 2.0, (1, I))).astype(np.float32),
        "base": (0.5 * n((Q, T))).astype(np.float32),
        "gq1": (np.random.uniform(0.3, 1.5, (Q, 1))).astype(np.float32),
        "offs": striped(idx),
    }


def reference(query, query2, keys_words, keys_scales, gout, vals_words, vals_scales, size, base, gq1, offs):
    idx = unstriped(offs)
    keysu = unpack_weight(keys_words, keys_scales, "e4m3")
    valsu = unpack_weight(vals_words, vals_scales, "e4m3")
    queryq = mxq(f64(query), 0, "e4m3")
    keysidxg = keysu[:, idx]
    a = queryq.T @ keysidxg
    query2q = mxq(f64(query2), 0, "e4m3")
    b = query2q.T @ keysidxg
    r = np.exp(a - np.max(a, axis=1, keepdims=True))
    gt = sigmoid(b)
    p = r * gt
    z = np.sum(p, axis=1, keepdims=True)
    goutq = mxq(f64(gout), 0, "e4m3")
    valsidxg = valsu[:, idx]
    c0 = goutq.T @ valsidxg
    dz = np.sum(c0 * p * f64(size) / np.square(z) * (-1.0), axis=1, keepdims=True)
    dp = c0 / z * f64(size) + dz
    dgt = dp * r
    db = dgt * gt * (1.0 - gt)
    hdb = db * 512.0 * 2.0 * 512.0
    hdgt = hdb * (1.0 - gt) * gt
    hdp = hdgt * r
    hdz = np.sum(hdp, axis=1, keepdims=True)
    hz = np.sum(hdp * f64(size) * c0 / np.square(z) * (-1.0), axis=1, keepdims=True) + np.sum(hdz * (-1.0) * c0 * p * f64(size) / np.square(np.square(z)) * (-1.0), axis=1, keepdims=True) * z * 2.0
    hp = hdz * (-1.0) / np.square(z) * c0 * f64(size) + hz
    hgt = hdb * (1.0 - gt) * dgt + hp * r - hdb * dgt * gt
    hb = hgt * gt * (1.0 - gt)
    gs = hb * f64(gq1)
    gf = np.zeros((Q, T))
    gf[:, idx] = gs
    y = f64(base) + gf
    return y

@@ -1,0 +1,197 @@
+from contextlib import ExitStack
+
+import concourse.mybir as mybir
+from concourse.masks import make_identity
+
+D, E, T, I, Q = 512, 512, 2048, 512, 128
+FLOPS = 3 * 2 * 512 * Q * I
+
+F32 = mybir.dt.float32
+BF16 = mybir.dt.bfloat16
+I32 = mybir.dt.int32
+U32 = mybir.dt.uint32
+U16 = mybir.dt.uint16
+U8 = mybir.dt.uint8
+FP8X4 = mybir.dt.float8_e4m3fn_x4
+ALU = mybir.AluOpType
+ACT = mybir.ActivationFunctionType
+
+P = 128
+PACK = 4
+ROOT = (512.0 * 2.0 * 512.0) ** (1.0 / 3.0)
+VALS_ROW = 4
+STORE_WIDTHS = (512, 512, 512, 512)
+HALVES = (slice(0, I // 2), slice(I // 2, I))
+
+
+def tile_attend_gpgatedexp_b_kernel(
+    tc, query, query2, keys_words, keys_scales, gout, vals_words, vals_scales, size, base, gq1, offs, out
+):
+    nc = tc.nc
+    with ExitStack() as ctx:
+        sb = ctx.enter_context(tc.tile_pool(name="sb", bufs=1))
+        ps = ctx.enter_context(tc.psum_pool(name="ps", bufs=1))
+
+        offsets = sb.tile([P, I // 16], U16, name="offsets")
+        nc.sync.dma_start(offsets[:], offs)
+
+        def zeroed_scale_window(name):
+            window = sb.tile([P, T], U8, name=name, align_bytes=64)
+            nc.vector.memset(window[:].bitcast(I32), 0)
+            return window
+
+        def load_scales(window, scales, first_row):
+            for a in range(4):
+                rows = slice(32 * a + first_row, 32 * a + first_row + 4)
+                nc.sync.dma_start(window[rows, :].bitcast(I32), scales[0, 4 * a : 4 * a + 4, :].bitcast(I32))
+
+        def load_words(name, words, tag):
+            window = sb.tile([P, T], I32, name=name, tag=tag, align_bytes=64)
+            nc.sync.dma_start(window[:], words[0].rearrange("p n t -> p (n t)").bitcast(I32))
+            return window
+
+        def load_rows(name, rows, tag):
+            raw = sb.tile([P, PACK, Q], F32, name=name, tag=tag, align_bytes=64)
+            nc.sync.dma_start(raw[:], rows.rearrange("(p j) q -> p j q", j=PACK))
+            return raw
+
+        def cast_on_scalar(dst, src):
+            nc.scalar.copy(dst, src)
+
+        def cast_on_gpsimd(dst, src):
+            nc.gpsimd.tensor_scalar(dst, src, 1.0, 0.0, ALU.mult, ALU.add)
+
+        def quantise(name, raw, cast, codes_tag):
+            grouped = sb.tile([P, Q, PACK], BF16, name=name + "_bf", align_bytes=64)
+            cast(grouped[:], raw[:].rearrange("p j q -> p q j"))
+            codes = sb.tile([P, Q], U32, name=name + "_codes", tag=codes_tag, align_bytes=64)
+            scales = sb.tile([P, Q], U8, name=name + "_scales", align_bytes=64)
+            nc.vector.quantize_mx(
+                out=codes[:].bitcast(FP8X4), scales=scales[:], in_=grouped[:].rearrange("p q j -> p (q j)")
+            )
+            return codes, scales
+
+        def gather(picked, window, slots):
+            nc.vector.tensor_copy(picked[:, slots], window.indirect(offsets[:, slots.start // 16 : slots.stop // 16]))
+
+        def product(bank, stationary, words, scales):
+            nc.tensor.matmul_mx(
+                out=bank,
+                lhsT=stationary[0][:].bitcast(FP8X4),
+                lhsT_scale=stationary[1][:],
+                rhs=words.bitcast(FP8X4),
+                rhs_scale=scales,
+                start=True,
+                stop=True,
+            )
+
+        def wide(name):
+            return sb.tile([Q, I], F32, name=name)
+
+        def column(name, tag=None):
+            return sb.tile([Q, 1], F32, name=name, tag=tag or name)
+
+        everything = slice(0, I)
+        ks_window = zeroed_scale_window("ks_window")
+        ident = sb.tile([P, P], F32, name="ident")
+        make_identity(nc, ident[:])
+        warm = sb.tile([Q, 1], F32, name="warm", tag="keys_slot", align_bytes=64)
+        nc.vector.memset(warm[:], 0.0)
+        warm_out = column("warm_out")
+        nc.scalar.activation(warm_out[:], warm[:], ACT.Sigmoid)
+        scattered = sb.tile([Q, T], F32, name="scattered")
+        nc.vector.memset(scattered[:], 0.0)
+        vs_window = zeroed_scale_window("vs_window")
+
+        q2_raw = load_rows("q2_raw", query2, "q2_raw")
+        q1_raw = load_rows("q1_raw", query, "q1_raw")
+        load_scales(ks_window, keys_scales, 0)
+        kw_window = load_words("kw_window", keys_words, "keys_slot")
+        load_scales(vs_window, vals_scales, VALS_ROW)
+        q2_mx = quantise("q2", q2_raw, cast_on_scalar, "q2_codes")
+        q1_mx = quantise("q1", q1_raw, cast_on_scalar, "q1_codes")
+        gout_raw = load_rows("gout_raw", gout, "q2_raw")
+        vw_window = load_words("vw_window", vals_words, "q1_raw")
+        ks = sb.tile([P, I], U8, name="ks", align_bytes=64)
+        gather(ks, ks_window[:], everything)
+        size4 = sb.tile([P, PACK], F32, name="size4", tag="q2_bf", align_bytes=64)
+        nc.scalar.dma_start(size4[:], size[0].rearrange("(p j) -> p j", j=PACK))
+        gq = sb.tile([Q, 1], F32, name="gq", tag="q1_bf", align_bytes=64)
+        nc.sync.dma_start(gq[:], gq1)
+
+        kw = sb.tile([P, I], U32, name="kw", align_bytes=64)
+        g = wide("g")
+        for n, half in enumerate(HALVES):
+            gather(kw, kw_window[:].bitcast(U32), half)
+            b = ps.tile([Q, I // 2], F32, name="b%d" % n)
+            product(b[:], q2_mx, kw[:, half], ks[:, half])
+            nc.scalar.activation(g[:, half], b[:], ACT.Sigmoid)
+        a = ps.tile([Q, I], F32, name="a")
+        product(a[:], q1_mx, kw[:], ks[:])
+
+        result = sb.tile([Q, T], F32, name="result", tag="q2_codes", align_bytes=64)
+        nc.sync.dma_start(result[:], base)
+
+        neg_max = column("neg_max")
+        nc.vector.tensor_reduce(neg_max[:], a[:], mybir.AxisListType.X, ALU.max, negate=True)
+        r = wide("r")
+        nc.scalar.activation(r[:], a[:], ACT.Exp, bias=neg_max[:])
+        size_bank = ps.tile([P, PACK, P], F32, name="size_bank", tag="b0")
+        for j in range(PACK):
+            nc.tensor.transpose(size_bank[:, j, :], size4[:, j : j + 1].to_broadcast([P, P]), ident[:])
+        after_exp = sb.tile([Q, 3 * I], F32, name="after_exp", tag="neg_max")
+        size_row, g_minus_one, slope = (after_exp[:, k * I : (k + 1) * I] for k in range(3))
+        nc.scalar.copy(size_row.rearrange("p (n j) -> p n j", j=PACK), size_bank[:].rearrange("p j n -> p n j"))
+        nc.scalar.activation(g_minus_one, g[:], ACT.Copy, scale=ROOT, bias=-ROOT)
+        nc.scalar.activation(slope, g[:], ACT.Copy, scale=-2.0 * ROOT, bias=ROOT)
+
+        vs = sb.tile([P, I], U8, name="vs", tag="keys_slot", align_bytes=64)
+        gather(vs, vs_window[:], everything)
+        gout_mx = quantise("gout", gout_raw, cast_on_gpsimd, "kw")
+        vw = sb.tile([P, I], U32, name="vw", tag="ks", align_bytes=64)
+        c0 = []
+        for n, half in enumerate(HALVES):
+            gather(vw, vw_window[:].bitcast(U32), half)
+            c0.append(ps.tile([Q, I // 2], F32, name="c0_%d" % n))
+            product(c0[n][:], gout_mx, vw[:, half], vs[VALS_ROW:P, half])
+
+        p = sb.tile([Q, I], F32, name="p", tag="q1_raw", align_bytes=64)
+        z = column("z")
+        nc.vector.scalar_tensor_tensor(p[:], r[:], 1.0, g[:], ALU.mult, ALU.mult, accum_out=z[:])
+        rz = column("rz")
+        nc.vector.reciprocal(rz[:], z[:])
+        c = wide("c")
+        for n, half in enumerate(HALVES):
+            nc.vector.tensor_tensor(c[:, half], c0[n][:], size_row[:, half], ALU.mult)
+        weighted = wide("weighted")
+        mean = column("mean")
+        nc.vector.scalar_tensor_tensor(weighted[:], p[:], rz[:], c[:], ALU.mult, ALU.mult, accum_out=mean[:])
+        u = wide("u")
+        db = wide("db")
+        for half in HALVES:
+            nc.vector.scalar_tensor_tensor(u[:, half], p[:, half], rz[:], g_minus_one[:, half], ALU.mult, ALU.mult)
+        for half in HALVES:
+            nc.vector.scalar_tensor_tensor(db[:, half], c[:, half], mean[:], u[:, half], ALU.subtract, ALU.mult)
+        u_gain = wide("u_gain")
+        nc.scalar.activation(u_gain[:], u[:], ACT.Copy, scale=gq[:])
+        db_sq = wide("db_sq")
+        sum_db_sq = column("sum_db_sq")
+        nc.scalar.activation(db_sq[:], db[:], ACT.Square, accum_out=sum_db_sq[:])
+        db_slope = wide("db_slope")
+        nc.vector.scalar_tensor_tensor(db_slope[:, HALVES[0]], db[:, HALVES[0]], gq[:], slope[:, HALVES[0]], ALU.mult, ALU.mult)
+        u_db = wide("u_db")
+        sum_u_db = column("sum_u_db")
+        nc.vector.scalar_tensor_tensor(u_db[:], u[:], gq[:], db[:], ALU.mult, ALU.mult, accum_out=sum_u_db[:])
+        nc.vector.scalar_tensor_tensor(db_slope[:, HALVES[1]], db[:, HALVES[1]], gq[:], slope[:, HALVES[1]], ALU.mult, ALU.mult)
+        term_u = wide("term_u")
+        nc.scalar.activation(term_u[:], u_gain[:], ACT.Copy, scale=sum_db_sq[:])
+        term_db = wide("term_db")
+        nc.vector.scalar_tensor_tensor(term_db[:], db_slope[:], sum_u_db[:], db[:], ALU.add, ALU.mult)
+        nc.vector.tensor_tensor(scattered[:].indirect(offsets[:]), term_db[:], term_u[:], ALU.add)
+
+        start = 0
+        for width in STORE_WIDTHS:
+            cols = slice(start, start + width)
+            nc.vector.tensor_tensor(result[:, cols], scattered[:, cols], result[:, cols], ALU.add)
+            nc.sync.dma_start(out[:, cols], result[:, cols])
+            start += width

@@ -20,7 +20,7 @@ P = 128
 PACK = 4
 ROOT = (512.0 * 2.0 * 512.0) ** (1.0 / 3.0)
 VALS_ROW = 4
-STORE_WIDTHS = (512, 512, 512, 512)
+STORE_WIDTHS = (256, 512, 512, 512, 256)
 HALVES = (slice(0, I // 2), slice(I // 2, I))
 
 
@@ -35,8 +35,8 @@ def tile_attend_gpgatedexp_b_kernel(
         offsets = sb.tile([P, I // 16], U16, name="offsets")
         nc.sync.dma_start(offsets[:], offs)
 
-        def zeroed_scale_window(name):
-            window = sb.tile([P, T], U8, name=name, align_bytes=64)
+        def zeroed_scale_window(name, tag):
+            window = sb.tile([P, T], U8, name=name, tag=tag, align_bytes=64)
             nc.vector.memset(window[:].bitcast(I32), 0)
             return window
 
@@ -92,32 +92,36 @@ def tile_attend_gpgatedexp_b_kernel(
             return sb.tile([Q, 1], F32, name=name, tag=tag or name)
 
         everything = slice(0, I)
-        ks_window = zeroed_scale_window("ks_window")
-        ident = sb.tile([P, P], F32, name="ident")
-        make_identity(nc, ident[:])
-        warm = sb.tile([Q, 1], F32, name="warm", tag="keys_slot", align_bytes=64)
-        nc.vector.memset(warm[:], 0.0)
+        ones = sb.tile([Q, 1], F32, name="ones", tag="keys_slot", align_bytes=64)
+        nc.vector.memset(ones[:], 1.0)
+        ks_window = zeroed_scale_window("ks_window", "ks_window")
+        root = column("root")
+        nc.vector.tensor_scalar(root[:], ones[:], ROOT, None, ALU.mult)
         warm_out = column("warm_out")
-        nc.scalar.activation(warm_out[:], warm[:], ACT.Sigmoid)
+        nc.scalar.activation(warm_out[:], root[:], ACT.Sigmoid)
         scattered = sb.tile([Q, T], F32, name="scattered")
         nc.vector.memset(scattered[:], 0.0)
-        vs_window = zeroed_scale_window("vs_window")
+        vs_window = zeroed_scale_window("vs_window", "vs_window")
+
+        size4 = sb.tile([P, PACK], F32, name="size4")
+        nc.gpsimd.dma_start(size4[:], size[0].rearrange("(p j) -> p j", j=PACK))
+        gq_tile = column("gq")
+        gq = gq_tile[:]
+        nc.gpsimd.dma_start(gq, gq1)
+        ident = sb.tile([P, P], F32, name="ident")
+        make_identity(nc, ident[:])
 
         q2_raw = load_rows("q2_raw", query2, "q2_raw")
         q1_raw = load_rows("q1_raw", query, "q1_raw")
         load_scales(ks_window, keys_scales, 0)
         kw_window = load_words("kw_window", keys_words, "keys_slot")
         load_scales(vs_window, vals_scales, VALS_ROW)
+        ks = sb.tile([P, I], U8, name="ks", align_bytes=64)
+        gather(ks, ks_window[:], everything)
         q2_mx = quantise("q2", q2_raw, cast_on_scalar, "q2_codes")
         q1_mx = quantise("q1", q1_raw, cast_on_scalar, "q1_codes")
         gout_raw = load_rows("gout_raw", gout, "q2_raw")
-        vw_window = load_words("vw_window", vals_words, "q1_raw")
-        ks = sb.tile([P, I], U8, name="ks", align_bytes=64)
-        gather(ks, ks_window[:], everything)
-        size4 = sb.tile([P, PACK], F32, name="size4", tag="q2_bf", align_bytes=64)
-        nc.scalar.dma_start(size4[:], size[0].rearrange("(p j) -> p j", j=PACK))
-        gq = sb.tile([Q, 1], F32, name="gq", tag="q1_bf", align_bytes=64)
-        nc.sync.dma_start(gq[:], gq1)
+        vw_window = load_words("vw_window", vals_words, "ks_window")
 
         kw = sb.tile([P, I], U32, name="kw", align_bytes=64)
         g = wide("g")
@@ -132,21 +136,21 @@ def tile_attend_gpgatedexp_b_kernel(
         result = sb.tile([Q, T], F32, name="result", tag="q2_codes", align_bytes=64)
         nc.sync.dma_start(result[:], base)
 
-        neg_max = column("neg_max")
+        vs = sb.tile([P, I], U8, name="vs", tag="keys_slot", align_bytes=64)
+        gather(vs, vs_window[:], everything)
+        neg_max = sb.tile([Q, 1], F32, name="neg_max", tag="vs_window", align_bytes=64)
         nc.vector.tensor_reduce(neg_max[:], a[:], mybir.AxisListType.X, ALU.max, negate=True)
         r = wide("r")
         nc.scalar.activation(r[:], a[:], ACT.Exp, bias=neg_max[:])
         size_bank = ps.tile([P, PACK, P], F32, name="size_bank", tag="b0")
         for j in range(PACK):
             nc.tensor.transpose(size_bank[:, j, :], size4[:, j : j + 1].to_broadcast([P, P]), ident[:])
-        after_exp = sb.tile([Q, 3 * I], F32, name="after_exp", tag="neg_max")
+        after_exp = sb.tile([Q, 3 * I], F32, name="after_exp", tag="vs_window", align_bytes=64)
         size_row, g_minus_one, slope = (after_exp[:, k * I : (k + 1) * I] for k in range(3))
         nc.scalar.copy(size_row.rearrange("p (n j) -> p n j", j=PACK), size_bank[:].rearrange("p j n -> p n j"))
         nc.scalar.activation(g_minus_one, g[:], ACT.Copy, scale=ROOT, bias=-ROOT)
-        nc.scalar.activation(slope, g[:], ACT.Copy, scale=-2.0 * ROOT, bias=ROOT)
+        nc.scalar.activation(slope, g[:], ACT.Identity, scale=-2.0 * ROOT, bias=root[:])
 
-        vs = sb.tile([P, I], U8, name="vs", tag="keys_slot", align_bytes=64)
-        gather(vs, vs_window[:], everything)
         gout_mx = quantise("gout", gout_raw, cast_on_gpsimd, "kw")
         vw = sb.tile([P, I], U32, name="vw", tag="ks", align_bytes=64)
         c0 = []
@@ -155,7 +159,7 @@ def tile_attend_gpgatedexp_b_kernel(
             c0.append(ps.tile([Q, I // 2], F32, name="c0_%d" % n))
             product(c0[n][:], gout_mx, vw[:, half], vs[VALS_ROW:P, half])
 
-        p = sb.tile([Q, I], F32, name="p", tag="q1_raw", align_bytes=64)
+        p = sb.tile([Q, I], F32, name="p", tag="ks_window", align_bytes=64)
         z = column("z")
         nc.vector.scalar_tensor_tensor(p[:], r[:], 1.0, g[:], ALU.mult, ALU.mult, accum_out=z[:])
         rz = column("rz")
@@ -173,16 +177,16 @@ def tile_attend_gpgatedexp_b_kernel(
         for half in HALVES:
             nc.vector.scalar_tensor_tensor(db[:, half], c[:, half], mean[:], u[:, half], ALU.subtract, ALU.mult)
         u_gain = wide("u_gain")
-        nc.scalar.activation(u_gain[:], u[:], ACT.Copy, scale=gq[:])
+        nc.scalar.activation(u_gain[:], u[:], ACT.Copy, scale=gq)
         db_sq = wide("db_sq")
         sum_db_sq = column("sum_db_sq")
         nc.scalar.activation(db_sq[:], db[:], ACT.Square, accum_out=sum_db_sq[:])
         db_slope = wide("db_slope")
-        nc.vector.scalar_tensor_tensor(db_slope[:, HALVES[0]], db[:, HALVES[0]], gq[:], slope[:, HALVES[0]], ALU.mult, ALU.mult)
+        nc.vector.scalar_tensor_tensor(db_slope[:, HALVES[0]], db[:, HALVES[0]], gq, slope[:, HALVES[0]], ALU.mult, ALU.mult)
         u_db = wide("u_db")
         sum_u_db = column("sum_u_db")
-        nc.vector.scalar_tensor_tensor(u_db[:], u[:], gq[:], db[:], ALU.mult, ALU.mult, accum_out=sum_u_db[:])
-        nc.vector.scalar_tensor_tensor(db_slope[:, HALVES[1]], db[:, HALVES[1]], gq[:], slope[:, HALVES[1]], ALU.mult, ALU.mult)
+        nc.vector.scalar_tensor_tensor(u_db[:], u[:], gq, db[:], ALU.mult, ALU.mult, accum_out=sum_u_db[:])
+        nc.vector.scalar_tensor_tensor(db_slope[:, HALVES[1]], db[:, HALVES[1]], gq, slope[:, HALVES[1]], ALU.mult, ALU.mult)
         term_u = wide("term_u")
         nc.scalar.activation(term_u[:], u_gain[:], ACT.Copy, scale=sum_db_sq[:])
         term_db = wide("term_db")

from contextlib import ExitStack

import concourse.mybir as mybir
from concourse.masks import make_identity

D, E, T, I, Q = 512, 512, 2048, 512, 128
FLOPS = 3 * 2 * 512 * Q * I

F32 = mybir.dt.float32
BF16 = mybir.dt.bfloat16
I32 = mybir.dt.int32
U32 = mybir.dt.uint32
U16 = mybir.dt.uint16
U8 = mybir.dt.uint8
FP8X4 = mybir.dt.float8_e4m3fn_x4
ALU = mybir.AluOpType
ACT = mybir.ActivationFunctionType

P = 128
PACK = 4
ROOT = (512.0 * 2.0 * 512.0) ** (1.0 / 3.0)
VALS_ROW = 4
STORE_WIDTHS = (256, 512, 512, 512, 256)
HALVES = (slice(0, I // 2), slice(I // 2, I))


def tile_attend_gpgatedexp_b_kernel(
    tc, query, query2, keys_words, keys_scales, gout, vals_words, vals_scales, size, base, gq1, offs, out
):
    nc = tc.nc
    with ExitStack() as ctx:
        sb = ctx.enter_context(tc.tile_pool(name="sb", bufs=1))
        ps = ctx.enter_context(tc.psum_pool(name="ps", bufs=1))

        offsets = sb.tile([P, I // 16], U16, name="offsets")
        nc.sync.dma_start(offsets[:], offs)

        def zeroed_scale_window(name, tag):
            window = sb.tile([P, T], U8, name=name, tag=tag, align_bytes=64)
            nc.vector.memset(window[:].bitcast(I32), 0)
            return window

        def load_scales(window, scales, first_row):
            for a in range(4):
                rows = slice(32 * a + first_row, 32 * a + first_row + 4)
                nc.sync.dma_start(window[rows, :].bitcast(I32), scales[0, 4 * a : 4 * a + 4, :].bitcast(I32))

        def load_words(name, words, tag):
            window = sb.tile([P, T], I32, name=name, tag=tag, align_bytes=64)
            nc.sync.dma_start(window[:], words[0].rearrange("p n t -> p (n t)").bitcast(I32))
            return window

        def load_rows(name, rows, tag):
            raw = sb.tile([P, PACK, Q], F32, name=name, tag=tag, align_bytes=64)
            nc.sync.dma_start(raw[:], rows.rearrange("(p j) q -> p j q", j=PACK))
            return raw

        def cast_on_scalar(dst, src):
            nc.scalar.copy(dst, src)

        def cast_on_gpsimd(dst, src):
            nc.gpsimd.tensor_scalar(dst, src, 1.0, 0.0, ALU.mult, ALU.add)

        def quantise(name, raw, cast, codes_tag):
            grouped = sb.tile([P, Q, PACK], BF16, name=name + "_bf", align_bytes=64)
            cast(grouped[:], raw[:].rearrange("p j q -> p q j"))
            codes = sb.tile([P, Q], U32, name=name + "_codes", tag=codes_tag, align_bytes=64)
            scales = sb.tile([P, Q], U8, name=name + "_scales", align_bytes=64)
            nc.vector.quantize_mx(
                out=codes[:].bitcast(FP8X4), scales=scales[:], in_=grouped[:].rearrange("p q j -> p (q j)")
            )
            return codes, scales

        def gather(picked, window, slots):
            nc.vector.tensor_copy(picked[:, slots], window.indirect(offsets[:, slots.start // 16 : slots.stop // 16]))

        def product(bank, stationary, words, scales):
            nc.tensor.matmul_mx(
                out=bank,
                lhsT=stationary[0][:].bitcast(FP8X4),
                lhsT_scale=stationary[1][:],
                rhs=words.bitcast(FP8X4),
                rhs_scale=scales,
                start=True,
                stop=True,
            )

        def wide(name):
            return sb.tile([Q, I], F32, name=name)

        def column(name, tag=None):
            return sb.tile([Q, 1], F32, name=name, tag=tag or name)

        everything = slice(0, I)
        ones = sb.tile([Q, 1], F32, name="ones", tag="keys_slot", align_bytes=64)
        nc.vector.memset(ones[:], 1.0)
        ks_window = zeroed_scale_window("ks_window", "ks_window")
        root = column("root")
        nc.vector.tensor_scalar(root[:], ones[:], ROOT, None, ALU.mult)
        warm_out = column("warm_out")
        nc.scalar.activation(warm_out[:], root[:], ACT.Sigmoid)
        scattered = sb.tile([Q, T], F32, name="scattered")
        nc.vector.memset(scattered[:], 0.0)
        vs_window = zeroed_scale_window("vs_window", "vs_window")

        size4 = sb.tile([P, PACK], F32, name="size4")
        nc.gpsimd.dma_start(size4[:], size[0].rearrange("(p j) -> p j", j=PACK))
        gq_tile = column("gq")
        gq = gq_tile[:]
        nc.gpsimd.dma_start(gq, gq1)
        ident = sb.tile([P, P], F32, name="ident")
        make_identity(nc, ident[:])

        q2_raw = load_rows("q2_raw", query2, "q2_raw")
        q1_raw = load_rows("q1_raw", query, "q1_raw")
        load_scales(ks_window, keys_scales, 0)
        kw_window = load_words("kw_window", keys_words, "keys_slot")
        load_scales(vs_window, vals_scales, VALS_ROW)
        ks = sb.tile([P, I], U8, name="ks", align_bytes=64)
        gather(ks, ks_window[:], everything)
        q2_mx = quantise("q2", q2_raw, cast_on_scalar, "q2_codes")
        q1_mx = quantise("q1", q1_raw, cast_on_scalar, "q1_codes")
        gout_raw = load_rows("gout_raw", gout, "q2_raw")
        vw_window = load_words("vw_window", vals_words, "ks_window")

        kw = sb.tile([P, I], U32, name="kw", align_bytes=64)
        g = wide("g")
        for n, half in enumerate(HALVES):
            gather(kw, kw_window[:].bitcast(U32), half)
            b = ps.tile([Q, I // 2], F32, name="b%d" % n)
            product(b[:], q2_mx, kw[:, half], ks[:, half])
            nc.scalar.activation(g[:, half], b[:], ACT.Sigmoid)
        a = ps.tile([Q, I], F32, name="a")
        product(a[:], q1_mx, kw[:], ks[:])

        result = sb.tile([Q, T], F32, name="result", tag="q2_codes", align_bytes=64)
        nc.sync.dma_start(result[:], base)

        vs = sb.tile([P, I], U8, name="vs", tag="keys_slot", align_bytes=64)
        gather(vs, vs_window[:], everything)
        neg_max = sb.tile([Q, 1], F32, name="neg_max", tag="vs_window", align_bytes=64)
        nc.vector.tensor_reduce(neg_max[:], a[:], mybir.AxisListType.X, ALU.max, negate=True)
        r = wide("r")
        nc.scalar.activation(r[:], a[:], ACT.Exp, bias=neg_max[:])
        size_bank = ps.tile([P, PACK, P], F32, name="size_bank", tag="b0")
        for j in range(PACK):
            nc.tensor.transpose(size_bank[:, j, :], size4[:, j : j + 1].to_broadcast([P, P]), ident[:])
        after_exp = sb.tile([Q, 3 * I], F32, name="after_exp", tag="vs_window", align_bytes=64)
        size_row, g_minus_one, slope = (after_exp[:, k * I : (k + 1) * I] for k in range(3))
        nc.scalar.copy(size_row.rearrange("p (n j) -> p n j", j=PACK), size_bank[:].rearrange("p j n -> p n j"))
        nc.scalar.activation(g_minus_one, g[:], ACT.Copy, scale=ROOT, bias=-ROOT)
        nc.scalar.activation(slope, g[:], ACT.Identity, scale=-2.0 * ROOT, bias=root[:])

        gout_mx = quantise("gout", gout_raw, cast_on_gpsimd, "kw")
        vw = sb.tile([P, I], U32, name="vw", tag="ks", align_bytes=64)
        c0 = []
        for n, half in enumerate(HALVES):
            gather(vw, vw_window[:].bitcast(U32), half)
            c0.append(ps.tile([Q, I // 2], F32, name="c0_%d" % n))
            product(c0[n][:], gout_mx, vw[:, half], vs[VALS_ROW:P, half])

        p = sb.tile([Q, I], F32, name="p", tag="ks_window", align_bytes=64)
        z = column("z")
        nc.vector.scalar_tensor_tensor(p[:], r[:], 1.0, g[:], ALU.mult, ALU.mult, accum_out=z[:])
        rz = column("rz")
        nc.vector.reciprocal(rz[:], z[:])
        c = wide("c")
        for n, half in enumerate(HALVES):
            nc.vector.tensor_tensor(c[:, half], c0[n][:], size_row[:, half], ALU.mult)
        weighted = wide("weighted")
        mean = column("mean")
        nc.vector.scalar_tensor_tensor(weighted[:], p[:], rz[:], c[:], ALU.mult, ALU.mult, accum_out=mean[:])
        u = wide("u")
        db = wide("db")
        for half in HALVES:
            nc.vector.scalar_tensor_tensor(u[:, half], p[:, half], rz[:], g_minus_one[:, half], ALU.mult, ALU.mult)
        for half in HALVES:
            nc.vector.scalar_tensor_tensor(db[:, half], c[:, half], mean[:], u[:, half], ALU.subtract, ALU.mult)
        u_gain = wide("u_gain")
        nc.scalar.activation(u_gain[:], u[:], ACT.Copy, scale=gq)
        db_sq = wide("db_sq")
        sum_db_sq = column("sum_db_sq")
        nc.scalar.activation(db_sq[:], db[:], ACT.Square, accum_out=sum_db_sq[:])
        db_slope = wide("db_slope")
        nc.vector.scalar_tensor_tensor(db_slope[:, HALVES[0]], db[:, HALVES[0]], gq, slope[:, HALVES[0]], ALU.mult, ALU.mult)
        u_db = wide("u_db")
        sum_u_db = column("sum_u_db")
        nc.vector.scalar_tensor_tensor(u_db[:], u[:], gq, db[:], ALU.mult, ALU.mult, accum_out=sum_u_db[:])
        nc.vector.scalar_tensor_tensor(db_slope[:, HALVES[1]], db[:, HALVES[1]], gq, slope[:, HALVES[1]], ALU.mult, ALU.mult)
        term_u = wide("term_u")
        nc.scalar.activation(term_u[:], u_gain[:], ACT.Copy, scale=sum_db_sq[:])
        term_db = wide("term_db")
        nc.vector.scalar_tensor_tensor(term_db[:], db_slope[:], sum_u_db[:], db[:], ALU.add, ALU.mult)
        nc.vector.tensor_tensor(scattered[:].indirect(offsets[:]), term_db[:], term_u[:], ALU.add)

        start = 0
        for width in STORE_WIDTHS:
            cols = slice(start, start + width)
            nc.vector.tensor_tensor(result[:, cols], scattered[:, cols], result[:, cols], ALU.add)
            nc.sync.dma_start(out[:, cols], result[:, cols])
            start += width
